import numpy as np
import ml_dtypes


def mxq(x, axis, fmt="e4m3"):
    dtype, down = {"e4m3": (ml_dtypes.float8_e4m3fn, 7), "e5m2": (ml_dtypes.float8_e5m2, 14)}[fmt]
    v = np.moveaxis(np.asarray(x, np.float32).astype(ml_dtypes.bfloat16).astype(np.float64), axis, -1)
    blocks = v.reshape(v.shape[:-1] + (-1, 32))
    amax = np.abs(blocks).max(-1, keepdims=True)
    byte = np.maximum(np.where(amax > 0, np.frexp(amax)[1] - 1 + 127, 0) - down, 1)
    scale = np.exp2(byte - 127.0)
    codes = (blocks / scale).astype(np.float32).astype(dtype).astype(np.float64)
    return np.moveaxis((codes * scale).reshape(v.shape), -1, axis)


WIDE = False


def mx_kscale(k):
    if not WIDE:
        return np.ones(k)
    levels = np.array([30, -30])
    if k % 512:
        return np.exp2(np.random.permutation(np.resize(levels, k // 32))).repeat(32)
    a = np.empty((k // 512, 16))
    for p in range(k // 512):
        a[p, :8] = np.random.permutation(np.resize(levels, 8))
        for g in range(8):
            far = levels[np.abs(levels - a[p, g]) >= 10]
            a[p, g + 8] = far[np.random.randint(len(far))]
    return np.exp2(a.ravel()).repeat(32)


def f64(x):
    return np.asarray(x).astype(np.float64)


def striped(idx):
    return np.tile(np.asarray(idx).reshape(-1, 16).T, (8, 1)).astype(np.uint16)


def unstriped(offs):
    return offs[:16].T.reshape(-1).astype(np.int64)


def striped8(idx):
    return np.asarray(idx).reshape(8, -1, 16).transpose(0, 2, 1).reshape(128, -1).astype(np.uint16)


def unstriped8(offs):
    return offs.reshape(8, 16, -1).transpose(0, 2, 1).reshape(8, -1).astype(np.int64)


def pick8(x, idx, run):
    r = np.arange(len(x))
    return x[r[:, None], idx[r % (8 * run) // run]]


E2M1 = np.array([0.0, 0.5, 1.0, 1.5, 2.0, 3.0, 4.0, 6.0, -0.0, -0.5, -1.0, -1.5, -2.0, -3.0, -4.0, -6.0])


def pack_weight(w, fmt):
    k, n = w.shape
    w = f64(np.asarray(w, np.float32).astype(ml_dtypes.bfloat16)).reshape(k // 32, 32, n)
    amax = np.abs(w).max(1)
    if fmt in ("e4m3", "e5m2"):
        byte = np.frexp(amax)[1] - 1 + 127 - (7 if fmt == "e4m3" else 14)
    else:
        mant, ex = np.frexp(amax / 6.0)
        byte = np.where(mant > 0.5, ex, ex - 1) + 127
    byte = np.clip(np.where(amax > 0, byte, 1), 1, 254)
    scaled = (w * np.exp2(127.0 - byte)[:, None, :]).reshape(k, n).astype(np.float32)
    by_word = np.ascontiguousarray(scaled.reshape(k // 512, 128, 4, n).transpose(0, 1, 3, 2))
    if fmt in ("e4m3", "e5m2"):
        words = by_word.astype(ml_dtypes.float8_e4m3fn if fmt == "e4m3" else ml_dtypes.float8_e5m2).view(np.uint8)
    else:
        c = by_word.astype(ml_dtypes.float4_e2m1fn).view(np.uint8) & 0xF
        words = (c[..., 0::2] | (c[..., 1::2] << 4)).reshape(k // 512, 128, 2 * n)
    return np.ascontiguousarray(words), np.ascontiguousarray(byte.astype(np.uint8).reshape(k // 512, 16, n))


def unpack_weight(words, scales, fmt):
    g, _, n = scales.shape
    words = np.ascontiguousarray(words).reshape(g, 128, n, -1)
    if fmt in ("e4m3", "e5m2"):
        vals = words.view(ml_dtypes.float8_e4m3fn if fmt == "e4m3" else ml_dtypes.float8_e5m2).astype(np.float64)
    else:
        nib = np.empty((g, 128, n, 4), np.uint8)
        nib[..., 0::2] = words & 0xF
        nib[..., 1::2] = words >> 4
        vals = E2M1[nib]
    vals = vals * np.repeat(np.exp2(scales.astype(np.float64) - 127.0), 8, axis=1)[..., None]
    return vals.transpose(0, 1, 3, 2).reshape(g * 512, n)


def e4m3fn_bytes(y):
    return np.clip(np.asarray(y, np.float64), -448.0, 448.0).astype(np.float32).astype(ml_dtypes.float8_e4m3fn).view(np.uint8)


def e4m3fn_values(b):
    return np.asarray(b, np.uint8).view(ml_dtypes.float8_e4m3fn).astype(np.float64)


K, T, J, R, V, N, E = 512, 1024, 256, 512, 1024, 256, 512


def setup_inputs():
    n = np.random.standard_normal
    idx = np.random.permutation(T)[:J]
    idx2 = np.stack([np.random.permutation(V)[:J] for _ in range(8)])
    idx3 = np.random.permutation(V)[:J]
    idx4 = np.random.permutation(E)[:J]
    fk = mx_kscale(K)
    fr = mx_kscale(R)
    xtp = pack_weight(n((K, T)) / fk[:, None], "e5m2")
    wp = pack_weight(n((K, R)) * 1 / np.sqrt(K) * fk[:, None], "e2m1")
    w2p = pack_weight(n((K, R)) * 1 / np.sqrt(K) * fk[:, None], "e4m3")
    wbp = pack_weight(n((R, N)) * 1 / np.sqrt(R) / fr[:, None], "e2m1")
    return {
        "xt_words": xtp[0],
        "xt_scales": xtp[1],
        "w_words": wp[0],
        "w_scales": wp[1],
        "w2_words": w2p[0],
        "w2_scales": w2p[1],
        "ca": e4m3fn_bytes(60.0 * n((R, V))),
        "sa": (np.random.uniform(0.004, 0.012, (R, 1)) * fr[:, None]).astype(np.float32),
        "sb": (np.random.uniform(0.004, 0.012, (R, 1)) * fr[:, None]).astype(np.float32),
        "wb_words": wbp[0],
        "wb_scales": wbp[1],
        "so": (np.random.uniform(0.5, 1.6, (N, 1))).astype(np.float32),
        "offs": striped(idx),
        "offs2": striped8(idx2),
        "offs3": striped(idx3),
        "offs4": striped(idx4),
    }


def reference(xt_words, xt_scales, w_words, w_scales, w2_words, w2_scales, ca, sa, sb, wb_words, wb_scales, so, offs, offs2, offs3, offs4):
    idx = unstriped(offs)
    idx2 = unstriped8(offs2)
    idx3 = unstriped(offs3)
    idx4 = unstriped(offs4)
    xtu = unpack_weight(xt_words, xt_scales, "e5m2")
    wu = unpack_weight(w_words, w_scales, "e2m1")
    w2u = unpack_weight(w2_words, w2_scales, "e4m3")
    wbu = unpack_weight(wb_words, wb_scales, "e2m1")
    xtidxg = xtu[:, idx]
    a = wu.T @ xtidxg
    b = w2u.T @ xtidxg
    ga = pick8(e4m3fn_values(ca), idx2, 64) * f64(sa)
    gb = e4m3fn_values(ca)[:, idx3] * f64(sb)
    hid = a * ga + b * gb
    hidq = mxq(hid, 0, "e4m3")
    p = wbu.T @ hidq
    y = np.zeros((N, E))
    y[:, idx4] = p * f64(so)
    return y

@@ -1,0 +1,172 @@
+from contextlib import ExitStack
+
+import concourse.mybir as mybir
+
+K, T, J, R, V, N, E = 512, 1024, 256, 512, 1024, 256, 512
+FLOPS = 2 * 2 * K * R * J + 2 * R * N * J
+
+F32 = mybir.dt.float32
+BF16 = mybir.dt.bfloat16
+I32 = mybir.dt.int32
+U32 = mybir.dt.uint32
+U16 = mybir.dt.uint16
+U8 = mybir.dt.uint8
+FP8 = mybir.dt.float8_e4m3fn
+E4M3X4 = mybir.dt.float8_e4m3fn_x4
+E5M2X4 = mybir.dt.float8_e5m2_x4
+E2M1X4 = mybir.dt.float4_e2m1fn_x4
+COPY = mybir.ActivationFunctionType.Copy
+MULT = mybir.AluOpType.mult
+ADD = mybir.AluOpType.add
+
+P = 128
+PACK = 4
+HALF = J // 2
+
+
+def tile_list_groupandcommon_kernel(tc, xt_words, xt_scales, w_words, w_scales, w2_words, w2_scales, ca, sa, sb,
+                                        wb_words, wb_scales, so, offs, offs2, offs3, offs4, out):
+    nc = tc.nc
+    with ExitStack() as ctx:
+        lists = ctx.enter_context(tc.tile_pool(name="lists", bufs=1))
+        sbuf = ctx.enter_context(tc.tile_pool(name="sbuf", bufs=1))
+        psum = ctx.enter_context(tc.psum_pool(name="psum", bufs=1))
+
+        def tile(name, shape, dtype):
+            return sbuf.tile(shape, dtype, name=name, align_bytes=64)
+
+        def list_tile(name):
+            return lists.tile([P, J // 16], U16, name=name)
+
+        xt_list, group_list, common_list, page_list = [list_tile(n) for n in ("xt_list", "group_list", "common_list", "page_list")]
+        store = [tile("store%d" % t, [P, V], U8) for t in range(PACK)]
+        xt_w = tile("xt_w", [P, T], I32)
+        xt_s = tile("xt_s", [P, T], U8)
+        w_w = tile("w_w", [P, 2 * R], U8)
+        w_s = tile("w_s", [P, R], U8)
+        w2_w = tile("w2_w", [P, R], I32)
+        w2_s = tile("w2_s", [P, R], U8)
+        wb_w = tile("wb_w", [P, 2 * N], U8)
+        wb_s = tile("wb_s", [P, N], U8)
+        sa_t = tile("sa_t", [P, PACK], F32)
+        sb_t = tile("sb_t", [P, PACK], F32)
+        so_t = tile("so_t", [P, N // P], F32)
+        page = [tile("page%d" % n, [P, E], F32) for n in range(N // P)]
+
+        for plane in (xt_s, w_s, w2_s, wb_s):
+            nc.vector.memset(plane[:].bitcast(I32), 0)
+        for n in range(N // P):
+            nc.vector.memset(page[n][:], 0.0)
+
+        def load_scales(plane, rows):
+            for q in range(4):
+                nc.sync.dma_start(plane[32 * q : 32 * q + 4, :].bitcast(I32), rows[0, 4 * q : 4 * q + 4, :].bitcast(I32))
+
+        ca_rows = ca.rearrange("(p t) v -> p t v", t=PACK)
+        nc.sync.dma_start(group_list[:], offs2)
+        nc.sync.dma_start(store[0][:], ca_rows[:, 0, :])
+        nc.sync.dma_start(common_list[:], offs3)
+        for t in range(1, PACK):
+            nc.sync.dma_start(store[t][:], ca_rows[:, t, :])
+        nc.sync.dma_start(xt_list[:], offs)
+        nc.sync.dma_start(xt_w[:], xt_words[0].rearrange("p c b -> p (c b)").bitcast(I32))
+        nc.sync.dma_start(w2_w[:], w2_words[0].rearrange("p c b -> p (c b)").bitcast(I32))
+        nc.sync.dma_start(w_w[:].bitcast(I32), w_words[0].bitcast(I32))
+        nc.sync.dma_start(sa_t[:], sa.rearrange("(p t) o -> p (t o)", t=PACK))
+        nc.sync.dma_start(sb_t[:], sb.rearrange("(p t) o -> p (t o)", t=PACK))
+        load_scales(xt_s, xt_scales)
+        load_scales(w_s, w_scales)
+        load_scales(w2_s, w2_scales)
+        nc.sync.dma_start(wb_w[:].bitcast(I32), wb_words[0].bitcast(I32))
+        load_scales(wb_s, wb_scales)
+        nc.sync.dma_start(page_list[:], offs4)
+        with nc.allow_non_contiguous_dma(reason="one float32 weight for each output row"):
+            nc.sync.dma_start(so_t[:], so.rearrange("(n p) o -> p (n o)", p=P))
+
+        ga = tile("ga", [P, PACK, J], F32)
+        gb = tile("gb", [P, PACK, J], F32)
+
+        def look_up(name, t, offsets, steps, gate):
+            codes = tile("%s%d" % (name, t), [P, J], U8)
+            nc.vector.tensor_copy(codes[:], store[t][:].indirect(offsets[:]))
+            nc.scalar.activation(gate[:, t, :], codes[:].bitcast(FP8), COPY, scale=steps[:, t : t + 1])
+
+        looks = [("ca", 0), ("cb", 0), ("ca", 1), ("cb", 1), ("ca", 2), ("cb", 2), ("ca", 3), ("cb", 3)]
+
+        def do_look(i):
+            name, t = looks[i]
+            if name == "ca":
+                look_up(name, t, group_list, sa_t, ga)
+            else:
+                look_up(name, t, common_list, sb_t, gb)
+
+        for i in range(5):
+            do_look(i)
+
+        w2_wp = tile("w2_wp", [P, R], U32)
+        nc.scalar.copy(w2_wp[:].rearrange("p (t m) -> p m t", t=PACK),
+                       w2_w[:].bitcast(U32).rearrange("p (m t) -> p m t", t=PACK))
+        w_wp = tile("w_wp", [P, 2 * R], U8)
+        nc.scalar.copy(w_wp[:].bitcast(U16).rearrange("p (t m) -> p t m", t=PACK),
+                       w_w[:].bitcast(U16).rearrange("p (m t) -> p t m", t=PACK))
+
+        xg_w = tile("xg_w", [P, J], U32)
+        xg_s = tile("xg_s", [P, J], U8)
+        nc.vector.tensor_copy(xg_w[:], xt_w[:].bitcast(U32).indirect(xt_list[:]))
+        nc.vector.tensor_copy(xg_s[:], xt_s[:].indirect(xt_list[:]))
+
+        def deal_scales(name, plane):
+            dealt = tile(name, [P, R], U8)
+            nc.vector.tensor_copy(dealt[:].rearrange("p (t m) -> p t m", t=PACK),
+                                  plane[:].rearrange("p (m t) -> p t m", t=PACK))
+            return dealt
+
+        do_look(5)
+        w_sp = deal_scales("w_sp", w_s)
+        do_look(6)
+        w2_sp = deal_scales("w2_sp", w2_s)
+        do_look(7)
+
+        a_ps, b_ps = [], []
+        for h in range(2):
+            cols = slice(h * HALF, (h + 1) * HALF)
+            a_bank = psum.tile([P, PACK, HALF], F32, name="a_bank%d" % h)
+            b_bank = psum.tile([P, PACK, HALF], F32, name="b_bank%d" % h)
+            for t in range(PACK):
+                nc.tensor.matmul_mx(out=a_bank[:, t, :], lhsT=w_wp[:, 2 * P * t : 2 * P * (t + 1)].bitcast(E2M1X4),
+                                    lhsT_scale=w_sp[:, P * t : P * (t + 1)], rhs=xg_w[:, cols].bitcast(E5M2X4),
+                                    rhs_scale=xg_s[:, cols], start=True, stop=True)
+            for t in range(PACK):
+                nc.tensor.matmul_mx(out=b_bank[:, t, :], lhsT=w2_wp[:, P * t : P * (t + 1)].bitcast(E4M3X4),
+                                    lhsT_scale=w2_sp[:, P * t : P * (t + 1)], rhs=xg_w[:, cols].bitcast(E5M2X4),
+                                    rhs_scale=xg_s[:, cols], start=True, stop=True)
+            a_ps.append(a_bank)
+            b_ps.append(b_bank)
+
+        for h in range(2):
+            cols = slice(h * HALF, (h + 1) * HALF)
+            first = tile("first%d" % h, [P, PACK, HALF], F32)
+            second = tile("second%d" % h, [P, PACK, HALF], F32)
+            nc.vector.tensor_tensor(first[:], a_ps[h][:], ga[:, :, cols], MULT)
+            nc.vector.tensor_tensor(second[:], b_ps[h][:], gb[:, :, cols], MULT)
+            hid = tile("hid%d" % h, [P, PACK * HALF], BF16)
+            nc.vector.tensor_tensor(hid[:].rearrange("p (c i t) -> p c t i", i=4, t=PACK),
+                                    first[:].rearrange("p t (c i) -> p c t i", i=4),
+                                    second[:].rearrange("p t (c i) -> p c t i", i=4), ADD)
+            hid_w = tile("hid_w%d" % h, [P, HALF], U32)
+            hid_s = tile("hid_s%d" % h, [P, HALF], U8)
+            nc.vector.quantize_mx(out=hid_w[:].bitcast(E4M3X4), scales=hid_s[:], in_=hid[:])
+            for n in range(N // P):
+                p_bank = psum.tile([P, HALF], F32, name="p_bank%d%d" % (h, n))
+                nc.tensor.matmul_mx(out=p_bank[:], lhsT=wb_w[:, 2 * P * n : 2 * P * (n + 1)].bitcast(E2M1X4),
+                                    lhsT_scale=wb_s[:, P * n : P * (n + 1)], rhs=hid_w[:].bitcast(E4M3X4),
+                                    rhs_scale=hid_s[:], start=True, stop=True)
+                p_rows = tile("p_rows%d%d" % (h, n), [P, HALF], F32)
+                if h == 0:
+                    nc.scalar.copy(p_rows[:], p_bank[:])
+                else:
+                    nc.vector.tensor_copy(p_rows[:], p_bank[:])
+                nc.scalar.activation(page[n][:].indirect(page_list[:, h * HALF // 16 : (h + 1) * HALF // 16]), p_rows[:],
+                                     COPY, scale=so_t[:, n : n + 1])
+        for n in range(N // P):
+            nc.sync.dma_start(out[n * P : (n + 1) * P, :], page[n][:])

@@ -32,8 +32,8 @@ def tile_list_groupandcommon_kernel(tc, xt_words, xt_scales, w_words, w_scales, 
         sbuf = ctx.enter_context(tc.tile_pool(name="sbuf", bufs=1))
         psum = ctx.enter_context(tc.psum_pool(name="psum", bufs=1))
 
-        def tile(name, shape, dtype):
-            return sbuf.tile(shape, dtype, name=name, align_bytes=64)
+        def tile(name, shape, dtype, tag=None):
+            return sbuf.tile(shape, dtype, name=name, tag=tag or name, align_bytes=64)
 
         def list_tile(name):
             return lists.tile([P, J // 16], U16, name=name)
@@ -58,57 +58,60 @@ def tile_list_groupandcommon_kernel(tc, xt_words, xt_scales, w_words, w_scales, 
         for n in range(N // P):
             nc.vector.memset(page[n][:], 0.0)
 
-        def load_scales(plane, rows):
-            for q in range(4):
+        def load_scales(plane, rows, q0, q1):
+            for q in range(q0, q1):
                 nc.sync.dma_start(plane[32 * q : 32 * q + 4, :].bitcast(I32), rows[0, 4 * q : 4 * q + 4, :].bitcast(I32))
+
+        nc.gpsimd.dma_start(sa_t[:], sa.rearrange("(p t) o -> p (t o)", t=PACK))
+        nc.gpsimd.dma_start(sb_t[:], sb.rearrange("(p t) o -> p (t o)", t=PACK))
+        with nc.allow_non_contiguous_dma(reason="one float32 weight for each output row"):
+            nc.gpsimd.dma_start(so_t[:], so.rearrange("(n p) o -> p (n o)", p=P))
 
         ca_rows = ca.rearrange("(p t) v -> p t v", t=PACK)
         nc.sync.dma_start(group_list[:], offs2)
         nc.sync.dma_start(store[0][:], ca_rows[:, 0, :])
         nc.sync.dma_start(common_list[:], offs3)
-        for t in range(1, PACK):
-            nc.sync.dma_start(store[t][:], ca_rows[:, t, :])
+        nc.sync.dma_start(store[1][:], ca_rows[:, 1, :])
         nc.sync.dma_start(xt_list[:], offs)
+        nc.sync.dma_start(store[2][:], ca_rows[:, 2, :])
+        nc.sync.dma_start(store[3][:], ca_rows[:, 3, :])
         nc.sync.dma_start(xt_w[:], xt_words[0].rearrange("p c b -> p (c b)").bitcast(I32))
-        nc.sync.dma_start(w2_w[:], w2_words[0].rearrange("p c b -> p (c b)").bitcast(I32))
+        load_scales(xt_s, xt_scales, 0, 4)
+        load_scales(w_s, w_scales, 0, 2)
         nc.sync.dma_start(w_w[:].bitcast(I32), w_words[0].bitcast(I32))
-        nc.sync.dma_start(sa_t[:], sa.rearrange("(p t) o -> p (t o)", t=PACK))
-        nc.sync.dma_start(sb_t[:], sb.rearrange("(p t) o -> p (t o)", t=PACK))
-        load_scales(xt_s, xt_scales)
-        load_scales(w_s, w_scales)
-        load_scales(w2_s, w2_scales)
+        nc.sync.dma_start(w2_w[:], w2_words[0].rearrange("p c b -> p (c b)").bitcast(I32))
+        load_scales(w_s, w_scales, 2, 4)
+        load_scales(w2_s, w2_scales, 0, 4)
         nc.sync.dma_start(wb_w[:].bitcast(I32), wb_words[0].bitcast(I32))
-        load_scales(wb_s, wb_scales)
         nc.sync.dma_start(page_list[:], offs4)
-        with nc.allow_non_contiguous_dma(reason="one float32 weight for each output row"):
-            nc.sync.dma_start(so_t[:], so.rearrange("(n p) o -> p (n o)", p=P))
+        load_scales(wb_s, wb_scales, 0, 4)
 
         ga = tile("ga", [P, PACK, J], F32)
         gb = tile("gb", [P, PACK, J], F32)
 
-        def look_up(name, t, offsets, steps, gate):
-            codes = tile("%s%d" % (name, t), [P, J], U8)
+        def look_up(name, t, offsets, steps, gate, tag):
+            codes = tile("%s%d" % (name, t), [P, J], U8, tag)
             nc.vector.tensor_copy(codes[:], store[t][:].indirect(offsets[:]))
             nc.scalar.activation(gate[:, t, :], codes[:].bitcast(FP8), COPY, scale=steps[:, t : t + 1])
 
         looks = [("ca", 0), ("cb", 0), ("ca", 1), ("cb", 1), ("ca", 2), ("cb", 2), ("ca", 3), ("cb", 3)]
 
-        def do_look(i):
+        def do_look(i, tag=None):
             name, t = looks[i]
             if name == "ca":
-                look_up(name, t, group_list, sa_t, ga)
+                look_up(name, t, group_list, sa_t, ga, tag)
             else:
-                look_up(name, t, common_list, sb_t, gb)
+                look_up(name, t, common_list, sb_t, gb, tag)
 
         for i in range(5):
             do_look(i)
 
-        w2_wp = tile("w2_wp", [P, R], U32)
-        nc.scalar.copy(w2_wp[:].rearrange("p (t m) -> p m t", t=PACK),
-                       w2_w[:].bitcast(U32).rearrange("p (m t) -> p m t", t=PACK))
         w_wp = tile("w_wp", [P, 2 * R], U8)
         nc.scalar.copy(w_wp[:].bitcast(U16).rearrange("p (t m) -> p t m", t=PACK),
                        w_w[:].bitcast(U16).rearrange("p (m t) -> p t m", t=PACK))
+        w2_wp = tile("w2_wp", [P, R], U32)
+        nc.scalar.copy(w2_wp[:].rearrange("p (t c m) -> p c t m", t=PACK, m=4),
+                       w2_w[:].bitcast(U32).rearrange("p (c m t) -> p c t m", t=PACK, m=4))
 
         xg_w = tile("xg_w", [P, J], U32)
         xg_s = tile("xg_s", [P, J], U8)
@@ -121,11 +124,11 @@ def tile_list_groupandcommon_kernel(tc, xt_words, xt_scales, w_words, w_scales, 
                                   plane[:].rearrange("p (m t) -> p t m", t=PACK))
             return dealt
 
-        do_look(5)
+        do_look(5, "xt_s")
         w_sp = deal_scales("w_sp", w_s)
-        do_look(6)
+        do_look(6, "w_s")
         w2_sp = deal_scales("w2_sp", w2_s)
-        do_look(7)
+        do_look(7, "w2_s")
 
         a_ps, b_ps = [], []
         for h in range(2):
@@ -145,14 +148,14 @@ def tile_list_groupandcommon_kernel(tc, xt_words, xt_scales, w_words, w_scales, 
 
         for h in range(2):
             cols = slice(h * HALF, (h + 1) * HALF)
-            first = tile("first%d" % h, [P, PACK, HALF], F32)
-            second = tile("second%d" % h, [P, PACK, HALF], F32)
+            first = tile("first%d" % h, [P, PACK, HALF], F32, "first")
+            second = tile("second%d" % h, [P, PACK, HALF], F32, "hid0" if h == 1 else None)
             nc.vector.tensor_tensor(first[:], a_ps[h][:], ga[:, :, cols], MULT)
             nc.vector.tensor_tensor(second[:], b_ps[h][:], gb[:, :, cols], MULT)
             hid = tile("hid%d" % h, [P, PACK * HALF], BF16)
-            nc.vector.tensor_tensor(hid[:].rearrange("p (c i t) -> p c t i", i=4, t=PACK),
-                                    first[:].rearrange("p t (c i) -> p c t i", i=4),
-                                    second[:].rearrange("p t (c i) -> p c t i", i=4), ADD)
+            nc.vector.tensor_tensor(hid[:].rearrange("p (c i t) -> p c t i", i=2, t=PACK),
+                                    first[:].rearrange("p t (c i) -> p c t i", i=2),
+                                    second[:].rearrange("p t (c i) -> p c t i", i=2), ADD)
             hid_w = tile("hid_w%d" % h, [P, HALF], U32)
             hid_s = tile("hid_s%d" % h, [P, HALF], U8)
             nc.vector.quantize_mx(out=hid_w[:].bitcast(E4M3X4), scales=hid_s[:], in_=hid[:])

@@ -46,77 +46,75 @@ def tile_list_groupandcommon_kernel(tc, xt_words, xt_scales, w_words, w_scales, 
         w_s = tile("w_s", [P, R], U8)
         w2_w = tile("w2_w", [P, R], I32)
         w2_s = tile("w2_s", [P, R], U8)
-        wb_w = tile("wb_w", [P, 2 * N], U8)
         wb_s = tile("wb_s", [P, N], U8)
         sa_t = tile("sa_t", [P, PACK], F32)
         sb_t = tile("sb_t", [P, PACK], F32)
-        so_t = tile("so_t", [P, N // P], F32)
         page = [tile("page%d" % n, [P, E], F32) for n in range(N // P)]
 
-        for plane in (xt_s, w_s, w2_s, wb_s):
+        nc.gpsimd.memset(w2_s[:].bitcast(I32), 0)
+        for plane in (xt_s, w_s, wb_s):
             nc.vector.memset(plane[:].bitcast(I32), 0)
         for n in range(N // P):
             nc.vector.memset(page[n][:], 0.0)
 
-        def load_scales(plane, rows, q0, q1):
-            for q in range(q0, q1):
-                nc.sync.dma_start(plane[32 * q : 32 * q + 4, :].bitcast(I32), rows[0, 4 * q : 4 * q + 4, :].bitcast(I32))
+        def load_scales(queue, plane, rows, quadrants=range(4)):
+            for q in quadrants:
+                queue.dma_start(plane[32 * q : 32 * q + 4, :].bitcast(I32), rows[0, 4 * q : 4 * q + 4, :].bitcast(I32))
 
-        nc.gpsimd.dma_start(sa_t[:], sa.rearrange("(p t) o -> p (t o)", t=PACK))
-        nc.gpsimd.dma_start(sb_t[:], sb.rearrange("(p t) o -> p (t o)", t=PACK))
-        with nc.allow_non_contiguous_dma(reason="one float32 weight for each output row"):
-            nc.gpsimd.dma_start(so_t[:], so.rearrange("(n p) o -> p (n o)", p=P))
+        load_scales(nc.gpsimd, w2_s, w2_scales, range(2, 4))
 
         ca_rows = ca.rearrange("(p t) v -> p t v", t=PACK)
         nc.sync.dma_start(group_list[:], offs2)
         nc.sync.dma_start(store[0][:], ca_rows[:, 0, :])
         nc.sync.dma_start(common_list[:], offs3)
         nc.sync.dma_start(store[1][:], ca_rows[:, 1, :])
-        nc.sync.dma_start(xt_list[:], offs)
+        nc.sync.dma_start(sa_t[:], sa.rearrange("(p t) o -> p (t o)", t=PACK))
         nc.sync.dma_start(store[2][:], ca_rows[:, 2, :])
         nc.sync.dma_start(store[3][:], ca_rows[:, 3, :])
-        nc.sync.dma_start(xt_w[:], xt_words[0].rearrange("p c b -> p (c b)").bitcast(I32))
-        load_scales(xt_s, xt_scales, 0, 4)
-        load_scales(w_s, w_scales, 0, 2)
         nc.sync.dma_start(w_w[:].bitcast(I32), w_words[0].bitcast(I32))
+        nc.sync.dma_start(xt_list[:], offs)
+        load_scales(nc.sync, xt_s, xt_scales)
+        nc.sync.dma_start(sb_t[:], sb.rearrange("(p t) o -> p (t o)", t=PACK))
+        nc.sync.dma_start(xt_w[:], xt_words[0].rearrange("p c b -> p (c b)").bitcast(I32))
         nc.sync.dma_start(w2_w[:], w2_words[0].rearrange("p c b -> p (c b)").bitcast(I32))
-        load_scales(w_s, w_scales, 2, 4)
-        load_scales(w2_s, w2_scales, 0, 4)
-        nc.sync.dma_start(wb_w[:].bitcast(I32), wb_words[0].bitcast(I32))
+        load_scales(nc.sync, w_s, w_scales)
+        load_scales(nc.sync, w2_s, w2_scales, range(2))
         nc.sync.dma_start(page_list[:], offs4)
-        load_scales(wb_s, wb_scales, 0, 4)
-
-        ga = tile("ga", [P, PACK, J], F32)
-        gb = tile("gb", [P, PACK, J], F32)
-
-        def look_up(name, t, offsets, steps, gate, tag):
-            codes = tile("%s%d" % (name, t), [P, J], U8, tag)
-            nc.vector.tensor_copy(codes[:], store[t][:].indirect(offsets[:]))
-            nc.scalar.activation(gate[:, t, :], codes[:].bitcast(FP8), COPY, scale=steps[:, t : t + 1])
-
-        looks = [("ca", 0), ("cb", 0), ("ca", 1), ("cb", 1), ("ca", 2), ("cb", 2), ("ca", 3), ("cb", 3)]
-
-        def do_look(i, tag=None):
-            name, t = looks[i]
-            if name == "ca":
-                look_up(name, t, group_list, sa_t, ga, tag)
-            else:
-                look_up(name, t, common_list, sb_t, gb, tag)
-
-        for i in range(5):
-            do_look(i)
+        load_scales(nc.sync, wb_s, wb_scales)
 
         w_wp = tile("w_wp", [P, 2 * R], U8)
         nc.scalar.copy(w_wp[:].bitcast(U16).rearrange("p (t m) -> p t m", t=PACK),
                        w_w[:].bitcast(U16).rearrange("p (m t) -> p t m", t=PACK))
+
+        ga = [tile("ga0", [P, PACK, HALF], F32), tile("ga1", [P, PACK, HALF], F32)]
+        gb = [tile("gb0", [P, PACK, HALF], F32), tile("gb1", [P, PACK, HALF], F32)]
+        uses = [(group_list, sa_t, ga), (common_list, sb_t, gb)]
+
+        def look_up(h, which, tag=None):
+            codes = tile("codes%d_%d" % (h, which[0]), [P, len(which), HALF], U8, tag)
+            for place, i in enumerate(which):
+                t = i // 2
+                offsets, steps, gate = uses[i % 2]
+                nc.vector.tensor_copy(codes[:, place, :], store[t][:].indirect(offsets[:, h * HALF // 16 : (h + 1) * HALF // 16]))
+                nc.scalar.activation(gate[h][:, t, :], codes[:, place, :].bitcast(FP8), COPY, scale=steps[:, t : t + 1])
+
+        look_up(0, range(8))
+
         w2_wp = tile("w2_wp", [P, R], U32)
         nc.scalar.copy(w2_wp[:].rearrange("p (t c m) -> p c t m", t=PACK, m=4),
                        w2_w[:].bitcast(U32).rearrange("p (c m t) -> p c t m", t=PACK, m=4))
 
         xg_w = tile("xg_w", [P, J], U32)
         xg_s = tile("xg_s", [P, J], U8)
-        nc.vector.tensor_copy(xg_w[:], xt_w[:].bitcast(U32).indirect(xt_list[:]))
         nc.vector.tensor_copy(xg_s[:], xt_s[:].indirect(xt_list[:]))
+        look_up(1, [0, 1], "xt_s")
+        nc.vector.tensor_copy(xg_w[:], xt_w[:].bitcast(U32).indirect(xt_list[:]))
+
+        wb_w = tile("wb_w", [P, 2 * N], U8, "codes0_0")
+        nc.sync.dma_start(wb_w[:].bitcast(I32), wb_words[0].bitcast(I32))
+        so_t = tile("so_t", [P, N // P], F32, "xt_w")
+        with nc.allow_non_contiguous_dma(reason="one float32 weight for each output row"):
+            nc.sync.dma_start(so_t[:], so.rearrange("(n p) o -> p (n o)", p=P))
 
         def deal_scales(name, plane):
             dealt = tile(name, [P, R], U8)
@@ -124,11 +122,9 @@ def tile_list_groupandcommon_kernel(tc, xt_words, xt_scales, w_words, w_scales, 
                                   plane[:].rearrange("p (m t) -> p t m", t=PACK))
             return dealt
 
-        do_look(5, "xt_s")
         w_sp = deal_scales("w_sp", w_s)
-        do_look(6, "w_s")
         w2_sp = deal_scales("w2_sp", w2_s)
-        do_look(7, "w2_s")
+        look_up(1, [2, 3], "w2_s")
 
         a_ps, b_ps = [], []
         for h in range(2):
@@ -146,30 +142,69 @@ def tile_list_groupandcommon_kernel(tc, xt_words, xt_scales, w_words, w_scales, 
             a_ps.append(a_bank)
             b_ps.append(b_bank)
 
-        for h in range(2):
-            cols = slice(h * HALF, (h + 1) * HALF)
-            first = tile("first%d" % h, [P, PACK, HALF], F32, "first")
-            second = tile("second%d" % h, [P, PACK, HALF], F32, "hid0" if h == 1 else None)
-            nc.vector.tensor_tensor(first[:], a_ps[h][:], ga[:, :, cols], MULT)
-            nc.vector.tensor_tensor(second[:], b_ps[h][:], gb[:, :, cols], MULT)
-            hid = tile("hid%d" % h, [P, PACK * HALF], BF16)
+        hid_w = tile("hid_w", [P, J], U32)
+        hid_s = tile("hid_s", [P, J], U8)
+
+        def product(name, j0, j1, banks, gate, tag=None):
+            h, lo, hi = j0 // HALF, j0 % HALF, (j1 - 1) % HALF + 1
+            prod = tile("%s%d" % (name, j0), [P, PACK, j1 - j0], F32, tag)
+            nc.vector.tensor_tensor(prod[:], banks[h][:, :, lo:hi], gate[h][:, :, lo:hi], MULT)
+            return prod
+
+        def add_up(j0, j1, first, second):
+            hid = tile("hid%d" % j0, [P, PACK * (j1 - j0)], BF16)
             nc.vector.tensor_tensor(hid[:].rearrange("p (c i t) -> p c t i", i=2, t=PACK),
                                     first[:].rearrange("p t (c i) -> p c t i", i=2),
                                     second[:].rearrange("p t (c i) -> p c t i", i=2), ADD)
-            hid_w = tile("hid_w%d" % h, [P, HALF], U32)
-            hid_s = tile("hid_s%d" % h, [P, HALF], U8)
-            nc.vector.quantize_mx(out=hid_w[:].bitcast(E4M3X4), scales=hid_s[:], in_=hid[:])
-            for n in range(N // P):
-                p_bank = psum.tile([P, HALF], F32, name="p_bank%d%d" % (h, n))
-                nc.tensor.matmul_mx(out=p_bank[:], lhsT=wb_w[:, 2 * P * n : 2 * P * (n + 1)].bitcast(E2M1X4),
-                                    lhsT_scale=wb_s[:, P * n : P * (n + 1)], rhs=hid_w[:].bitcast(E4M3X4),
-                                    rhs_scale=hid_s[:], start=True, stop=True)
-                p_rows = tile("p_rows%d%d" % (h, n), [P, HALF], F32)
-                if h == 0:
-                    nc.scalar.copy(p_rows[:], p_bank[:])
-                else:
-                    nc.vector.tensor_copy(p_rows[:], p_bank[:])
-                nc.scalar.activation(page[n][:].indirect(page_list[:, h * HALF // 16 : (h + 1) * HALF // 16]), p_rows[:],
-                                     COPY, scale=so_t[:, n : n + 1])
+            return hid
+
+        def quantise(j0, j1, hid):
+            nc.vector.quantize_mx(out=hid_w[:, j0:j1].bitcast(E4M3X4), scales=hid_s[:, j0:j1], in_=hid[:])
+
+        def project(bank, n, j1):
+            nc.tensor.matmul_mx(out=bank, lhsT=wb_w[:, 2 * P * n : 2 * P * (n + 1)].bitcast(E2M1X4),
+                                lhsT_scale=wb_s[:, P * n : P * (n + 1)], rhs=hid_w[:, j1 - HALF : j1].bitcast(E4M3X4),
+                                rhs_scale=hid_s[:, j1 - HALF : j1], start=True, stop=True)
+
+        def put(n, j0, j1, rows):
+            nc.scalar.activation(page[n][:].indirect(page_list[:, j0 // 16 : j1 // 16]), rows, COPY, scale=so_t[:, n : n + 1])
+
+        first = product("first", 0, 128, a_ps, ga, "store1")
+        second = product("second", 0, 128, b_ps, gb)
+        look_up(1, [4], "ga0")
+        hid = add_up(0, 128, first, second)
+        look_up(1, [5], "gb0")
+        quantise(0, 128, hid)
+        look_up(1, [6, 7], "store1")
+        bank = psum.tile([P, 2, HALF], F32, name="p_bank0")
+        rows = tile("p_rows0", [P, 2, HALF], F32)
+        for n in range(2):
+            project(bank[:, n, :], n, 128)
+        nc.scalar.copy(rows[:], bank[:])
+        for n in range(2):
+            put(n, 0, 128, rows[:, n, :])
+
+        first_b = product("first", 128, 192, a_ps, ga)
+        second_b = product("second", 128, 192, b_ps, gb)
+        first_c = product("first", 192, 256, a_ps, ga)
+        hid_b = add_up(128, 192, first_b, second_b)
+        second_c = product("second", 192, 256, b_ps, gb)
+        quantise(128, 192, hid_b)
+        hid_c = add_up(192, 256, first_c, second_c)
+        quantise(192, 256, hid_c)
+
+        bank = psum.tile([P, 2, HALF], F32, name="p_bank1")
+        rows = tile("p_rows1", [P, 2, 64], F32)
+        for n in range(2):
+            project(bank[:, n, :], n, 192)
+        nc.vector.tensor_copy(rows[:], bank[:, :, 64:128])
+        for n in range(2):
+            put(n, 128, 192, rows[:, n, :])
+        for n in range(2):
+            bank = psum.tile([P, HALF], F32, name="p_bank2%d" % n)
+            rows = tile("p_rows2%d" % n, [P, 64], F32)
+            project(bank[:], n, 256)
+            nc.vector.tensor_copy(rows[:], bank[:, 64:128])
+            put(n, 192, 256, rows[:])
         for n in range(N // P):
             nc.sync.dma_start(out[n * P : (n + 1) * P, :], page[n][:])

from contextlib import ExitStack

import concourse.mybir as mybir

K, T, J, R, V, N, E = 512, 1024, 256, 512, 1024, 256, 512
FLOPS = 2 * 2 * K * R * J + 2 * R * N * J

F32 = mybir.dt.float32
BF16 = mybir.dt.bfloat16
I32 = mybir.dt.int32
U32 = mybir.dt.uint32
U16 = mybir.dt.uint16
U8 = mybir.dt.uint8
FP8 = mybir.dt.float8_e4m3fn
E4M3X4 = mybir.dt.float8_e4m3fn_x4
E5M2X4 = mybir.dt.float8_e5m2_x4
E2M1X4 = mybir.dt.float4_e2m1fn_x4
COPY = mybir.ActivationFunctionType.Copy
MULT = mybir.AluOpType.mult
ADD = mybir.AluOpType.add

P = 128
PACK = 4
HALF = J // 2


def tile_list_groupandcommon_kernel(tc, xt_words, xt_scales, w_words, w_scales, w2_words, w2_scales, ca, sa, sb,
                                        wb_words, wb_scales, so, offs, offs2, offs3, offs4, out):
    nc = tc.nc
    with ExitStack() as ctx:
        lists = ctx.enter_context(tc.tile_pool(name="lists", bufs=1))
        sbuf = ctx.enter_context(tc.tile_pool(name="sbuf", bufs=1))
        psum = ctx.enter_context(tc.psum_pool(name="psum", bufs=1))

        def tile(name, shape, dtype, tag=None):
            return sbuf.tile(shape, dtype, name=name, tag=tag or name, align_bytes=64)

        def list_tile(name):
            return lists.tile([P, J // 16], U16, name=name)

        xt_list, group_list, common_list, page_list = [list_tile(n) for n in ("xt_list", "group_list", "common_list", "page_list")]
        store = [tile("store%d" % t, [P, V], U8) for t in range(PACK)]
        xt_w = tile("xt_w", [P, T], I32)
        xt_s = tile("xt_s", [P, T], U8)
        w_w = tile("w_w", [P, 2 * R], U8)
        w_s = tile("w_s", [P, R], U8)
        w2_w = tile("w2_w", [P, R], I32)
        w2_s = tile("w2_s", [P, R], U8)
        wb_s = tile("wb_s", [P, N], U8)
        sa_t = tile("sa_t", [P, PACK], F32)
        sb_t = tile("sb_t", [P, PACK], F32)
        page = [tile("page%d" % n, [P, E], F32) for n in range(N // P)]

        nc.gpsimd.memset(w2_s[:].bitcast(I32), 0)
        for plane in (xt_s, w_s, wb_s):
            nc.vector.memset(plane[:].bitcast(I32), 0)
        for n in range(N // P):
            nc.vector.memset(page[n][:], 0.0)

        def load_scales(queue, plane, rows, quadrants=range(4)):
            for q in quadrants:
                queue.dma_start(plane[32 * q : 32 * q + 4, :].bitcast(I32), rows[0, 4 * q : 4 * q + 4, :].bitcast(I32))

        load_scales(nc.gpsimd, w2_s, w2_scales, range(2, 4))

        ca_rows = ca.rearrange("(p t) v -> p t v", t=PACK)
        nc.sync.dma_start(group_list[:], offs2)
        nc.sync.dma_start(store[0][:], ca_rows[:, 0, :])
        nc.sync.dma_start(common_list[:], offs3)
        nc.sync.dma_start(store[1][:], ca_rows[:, 1, :])
        nc.sync.dma_start(sa_t[:], sa.rearrange("(p t) o -> p (t o)", t=PACK))
        nc.sync.dma_start(store[2][:], ca_rows[:, 2, :])
        nc.sync.dma_start(store[3][:], ca_rows[:, 3, :])
        nc.sync.dma_start(w_w[:].bitcast(I32), w_words[0].bitcast(I32))
        nc.sync.dma_start(xt_list[:], offs)
        load_scales(nc.sync, xt_s, xt_scales)
        nc.sync.dma_start(sb_t[:], sb.rearrange("(p t) o -> p (t o)", t=PACK))
        nc.sync.dma_start(xt_w[:], xt_words[0].rearrange("p c b -> p (c b)").bitcast(I32))
        nc.sync.dma_start(w2_w[:], w2_words[0].rearrange("p c b -> p (c b)").bitcast(I32))
        load_scales(nc.sync, w_s, w_scales)
        load_scales(nc.sync, w2_s, w2_scales, range(2))
        nc.sync.dma_start(page_list[:], offs4)
        load_scales(nc.sync, wb_s, wb_scales)

        w_wp = tile("w_wp", [P, 2 * R], U8)
        nc.scalar.copy(w_wp[:].bitcast(U16).rearrange("p (t m) -> p t m", t=PACK),
                       w_w[:].bitcast(U16).rearrange("p (m t) -> p t m", t=PACK))

        ga = [tile("ga0", [P, PACK, HALF], F32), tile("ga1", [P, PACK, HALF], F32)]
        gb = [tile("gb0", [P, PACK, HALF], F32), tile("gb1", [P, PACK, HALF], F32)]
        uses = [(group_list, sa_t, ga), (common_list, sb_t, gb)]

        def look_up(h, which, tag=None):
            codes = tile("codes%d_%d" % (h, which[0]), [P, len(which), HALF], U8, tag)
            for place, i in enumerate(which):
                t = i // 2
                offsets, steps, gate = uses[i % 2]
                nc.vector.tensor_copy(codes[:, place, :], store[t][:].indirect(offsets[:, h * HALF // 16 : (h + 1) * HALF // 16]))
                nc.scalar.activation(gate[h][:, t, :], codes[:, place, :].bitcast(FP8), COPY, scale=steps[:, t : t + 1])

        look_up(0, range(8))

        w2_wp = tile("w2_wp", [P, R], U32)
        nc.scalar.copy(w2_wp[:].rearrange("p (t c m) -> p c t m", t=PACK, m=4),
                       w2_w[:].bitcast(U32).rearrange("p (c m t) -> p c t m", t=PACK, m=4))

        xg_w = tile("xg_w", [P, J], U32)
        xg_s = tile("xg_s", [P, J], U8)
        nc.vector.tensor_copy(xg_s[:], xt_s[:].indirect(xt_list[:]))
        look_up(1, [0, 1], "xt_s")
        nc.vector.tensor_copy(xg_w[:], xt_w[:].bitcast(U32).indirect(xt_list[:]))

        wb_w = tile("wb_w", [P, 2 * N], U8, "codes0_0")
        nc.sync.dma_start(wb_w[:].bitcast(I32), wb_words[0].bitcast(I32))
        so_t = tile("so_t", [P, N // P], F32, "xt_w")
        with nc.allow_non_contiguous_dma(reason="one float32 weight for each output row"):
            nc.sync.dma_start(so_t[:], so.rearrange("(n p) o -> p (n o)", p=P))

        def deal_scales(name, plane):
            dealt = tile(name, [P, R], U8)
            nc.vector.tensor_copy(dealt[:].rearrange("p (t m) -> p t m", t=PACK),
                                  plane[:].rearrange("p (m t) -> p t m", t=PACK))
            return dealt

        w_sp = deal_scales("w_sp", w_s)
        w2_sp = deal_scales("w2_sp", w2_s)
        look_up(1, [2, 3], "w2_s")

        a_ps, b_ps = [], []
        for h in range(2):
            cols = slice(h * HALF, (h + 1) * HALF)
            a_bank = psum.tile([P, PACK, HALF], F32, name="a_bank%d" % h)
            b_bank = psum.tile([P, PACK, HALF], F32, name="b_bank%d" % h)
            for t in range(PACK):
                nc.tensor.matmul_mx(out=a_bank[:, t, :], lhsT=w_wp[:, 2 * P * t : 2 * P * (t + 1)].bitcast(E2M1X4),
                                    lhsT_scale=w_sp[:, P * t : P * (t + 1)], rhs=xg_w[:, cols].bitcast(E5M2X4),
                                    rhs_scale=xg_s[:, cols], start=True, stop=True)
            for t in range(PACK):
                nc.tensor.matmul_mx(out=b_bank[:, t, :], lhsT=w2_wp[:, P * t : P * (t + 1)].bitcast(E4M3X4),
                                    lhsT_scale=w2_sp[:, P * t : P * (t + 1)], rhs=xg_w[:, cols].bitcast(E5M2X4),
                                    rhs_scale=xg_s[:, cols], start=True, stop=True)
            a_ps.append(a_bank)
            b_ps.append(b_bank)

        hid_w = tile("hid_w", [P, J], U32)
        hid_s = tile("hid_s", [P, J], U8)

        def product(name, j0, j1, banks, gate, tag=None):
            h, lo, hi = j0 // HALF, j0 % HALF, (j1 - 1) % HALF + 1
            prod = tile("%s%d" % (name, j0), [P, PACK, j1 - j0], F32, tag)
            nc.vector.tensor_tensor(prod[:], banks[h][:, :, lo:hi], gate[h][:, :, lo:hi], MULT)
            return prod

        def add_up(j0, j1, first, second):
            hid = tile("hid%d" % j0, [P, PACK * (j1 - j0)], BF16)
            nc.vector.tensor_tensor(hid[:].rearrange("p (c i t) -> p c t i", i=2, t=PACK),
                                    first[:].rearrange("p t (c i) -> p c t i", i=2),
                                    second[:].rearrange("p t (c i) -> p c t i", i=2), ADD)
            return hid

        def quantise(j0, j1, hid):
            nc.vector.quantize_mx(out=hid_w[:, j0:j1].bitcast(E4M3X4), scales=hid_s[:, j0:j1], in_=hid[:])

        def project(bank, n, j1):
            nc.tensor.matmul_mx(out=bank, lhsT=wb_w[:, 2 * P * n : 2 * P * (n + 1)].bitcast(E2M1X4),
                                lhsT_scale=wb_s[:, P * n : P * (n + 1)], rhs=hid_w[:, j1 - HALF : j1].bitcast(E4M3X4),
                                rhs_scale=hid_s[:, j1 - HALF : j1], start=True, stop=True)

        def put(n, j0, j1, rows):
            nc.scalar.activation(page[n][:].indirect(page_list[:, j0 // 16 : j1 // 16]), rows, COPY, scale=so_t[:, n : n + 1])

        first = product("first", 0, 128, a_ps, ga, "store1")
        second = product("second", 0, 128, b_ps, gb)
        look_up(1, [4], "ga0")
        hid = add_up(0, 128, first, second)
        look_up(1, [5], "gb0")
        quantise(0, 128, hid)
        look_up(1, [6, 7], "store1")
        bank = psum.tile([P, 2, HALF], F32, name="p_bank0")
        rows = tile("p_rows0", [P, 2, HALF], F32)
        for n in range(2):
            project(bank[:, n, :], n, 128)
        nc.scalar.copy(rows[:], bank[:])
        for n in range(2):
            put(n, 0, 128, rows[:, n, :])

        first_b = product("first", 128, 192, a_ps, ga)
        second_b = product("second", 128, 192, b_ps, gb)
        first_c = product("first", 192, 256, a_ps, ga)
        hid_b = add_up(128, 192, first_b, second_b)
        second_c = product("second", 192, 256, b_ps, gb)
        quantise(128, 192, hid_b)
        hid_c = add_up(192, 256, first_c, second_c)
        quantise(192, 256, hid_c)

        bank = psum.tile([P, 2, HALF], F32, name="p_bank1")
        rows = tile("p_rows1", [P, 2, 64], F32)
        for n in range(2):
            project(bank[:, n, :], n, 192)
        nc.vector.tensor_copy(rows[:], bank[:, :, 64:128])
        for n in range(2):
            put(n, 128, 192, rows[:, n, :])
        for n in range(2):
            bank = psum.tile([P, HALF], F32, name="p_bank2%d" % n)
            rows = tile("p_rows2%d" % n, [P, 64], F32)
            project(bank[:], n, 256)
            nc.vector.tensor_copy(rows[:], bank[:, 64:128])
            put(n, 192, 256, rows[:])
        for n in range(N // P):
            nc.sync.dma_start(out[n * P : (n + 1) * P, :], page[n][:])
